import numpy as np
import ml_dtypes


def mxq(x, axis, fmt="e4m3"):
    dtype, down = {"e4m3": (ml_dtypes.float8_e4m3fn, 7), "e5m2": (ml_dtypes.float8_e5m2, 14)}[fmt]
    v = np.moveaxis(np.asarray(x, np.float32).astype(ml_dtypes.bfloat16).astype(np.float64), axis, -1)
    blocks = v.reshape(v.shape[:-1] + (-1, 32))
    amax = np.abs(blocks).max(-1, keepdims=True)
    byte = np.maximum(np.where(amax > 0, np.frexp(amax)[1] - 1 + 127, 0) - down, 1)
    scale = np.exp2(byte - 127.0)
    codes = (blocks / scale).astype(np.float32).astype(dtype).astype(np.float64)
    return np.moveaxis((codes * scale).reshape(v.shape), -1, axis)


WIDE = False


def mx_kscale(k):
    if not WIDE:
        return np.ones(k)
    levels = np.array([10, -10, 5, -5, 0])
    if k % 512:
        return np.exp2(np.random.permutation(np.resize(levels, k // 32))).repeat(32)
    a = np.empty((k // 512, 16))
    for p in range(k // 512):
        a[p, :8] = np.random.permutation(np.resize(levels, 8))
        for g in range(8):
            far = levels[np.abs(levels - a[p, g]) >= 10]
            a[p, g + 8] = far[np.random.randint(len(far))]
    return np.exp2(a.ravel()).repeat(32)


def f64(x):
    return np.asarray(x).astype(np.float64)


def striped(idx):
    return np.tile(np.asarray(idx).reshape(-1, 16).T, (8, 1)).astype(np.uint16)


def unstriped(offs):
    return offs[:16].T.reshape(-1).astype(np.int64)


E2M1 = np.array([0.0, 0.5, 1.0, 1.5, 2.0, 3.0, 4.0, 6.0, -0.0, -0.5, -1.0, -1.5, -2.0, -3.0, -4.0, -6.0])


def pack_weight(w, fmt):
    k, n = w.shape
    w = f64(np.asarray(w, np.float32).astype(ml_dtypes.bfloat16)).reshape(k // 32, 32, n)
    amax = np.abs(w).max(1)
    if fmt == "e4m3":
        byte = np.frexp(amax)[1] - 1 + 127 - 7
    else:
        mant, ex = np.frexp(amax / 6.0)
        byte = np.where(mant > 0.5, ex, ex - 1) + 127
    byte = np.clip(np.where(amax > 0, byte, 1), 1, 254)
    scaled = (w * np.exp2(127.0 - byte)[:, None, :]).reshape(k, n).astype(np.float32)
    by_word = np.ascontiguousarray(scaled.reshape(k // 512, 128, 4, n).transpose(0, 1, 3, 2))
    if fmt == "e4m3":
        words = by_word.astype(ml_dtypes.float8_e4m3fn).view(np.uint8)
    else:
        c = by_word.astype(ml_dtypes.float4_e2m1fn).view(np.uint8) & 0xF
        words = (c[..., 0::2] | (c[..., 1::2] << 4)).reshape(k // 512, 128, 2 * n)
    return np.ascontiguousarray(words), np.ascontiguousarray(byte.astype(np.uint8).reshape(k // 512, 16, n))


def unpack_weight(words, scales, fmt):
    g, _, n = scales.shape
    words = np.ascontiguousarray(words).reshape(g, 128, n, -1)
    if fmt == "e4m3":
        vals = words.view(ml_dtypes.float8_e4m3fn).astype(np.float64)
    else:
        nib = np.empty((g, 128, n, 4), np.uint8)
        nib[..., 0::2] = words & 0xF
        nib[..., 1::2] = words >> 4
        vals = E2M1[nib]
    vals = vals * np.repeat(np.exp2(scales.astype(np.float64) - 127.0), 8, axis=1)[..., None]
    return vals.transpose(0, 1, 3, 2).reshape(g * 512, n)


K, T, C, J, N = 512, 512, 2048, 512, 512


def setup_inputs():
    n = np.random.standard_normal
    idx = np.random.permutation(C)[:J]
    fk = mx_kscale(K)
    fj = mx_kscale(J)
    xtp = pack_weight(n((K, T)) * 0.3 / fk[:, None], "e4m3")
    wcp = pack_weight(n((K, C)) * 1 / np.sqrt(K) * fk[:, None], "e2m1")
    wop = pack_weight(n((J, N)) * 1 / np.sqrt(J) / fj[:, None], "e4m3")
    wsp = pack_weight(n((K, N)) * 1 / np.sqrt(K) * fk[:, None], "e2m1")
    return {
        "xt_words": xtp[0],
        "xt_scales": xtp[1],
        "wc_words": wcp[0],
        "wc_scales": wcp[1],
        "fj": (np.random.uniform(64.0, 128.0, (J, 1)) * fj[:, None]).astype(np.float32),
        "wo_words": wop[0],
        "wo_scales": wop[1],
        "ws_words": wsp[0],
        "ws_scales": wsp[1],
        "offs": striped(idx),
    }


def reference(xt_words, xt_scales, wc_words, wc_scales, fj, wo_words, wo_scales, ws_words, ws_scales, offs):
    idx = unstriped(offs)
    xtu = unpack_weight(xt_words, xt_scales, "e4m3")
    wcu = unpack_weight(wc_words, wc_scales, "e2m1")
    wou = unpack_weight(wo_words, wo_scales, "e4m3")
    wsu = unpack_weight(ws_words, ws_scales, "e2m1")
    wcidxg = wcu[:, idx]
    z = xtu.T @ wcidxg
    p = np.exp(z)
    q = p / np.sum(p, axis=1, keepdims=True)
    qt = q.T
    qw = qt * f64(fj)
    qwq = mxq(qw, 0, "e4m3")
    y = wou.T @ qwq + wsu.T @ xtu
    return y

@@ -1,0 +1,178 @@
+from contextlib import ExitStack
+
+import concourse.mybir as mybir
+from concourse.masks import make_identity
+
+K, T, C, J, N = 512, 512, 2048, 512, 512
+FLOPS = 2 * K * T * J + 2 * J * N * T + 2 * K * N * T
+
+F32 = mybir.dt.float32
+BF16 = mybir.dt.bfloat16
+I32 = mybir.dt.int32
+U32 = mybir.dt.uint32
+U16 = mybir.dt.uint16
+U8 = mybir.dt.uint8
+FP8X4 = mybir.dt.float8_e4m3fn_x4
+FP4X4 = mybir.dt.float4_e2m1fn_x4
+ACT = mybir.ActivationFunctionType
+ALU = mybir.AluOpType
+AXIS = mybir.AxisListType
+
+P = 128
+BLOCKS = T // P
+
+
+def load_scale_rows(queue, plane, rows, quads):
+    for quad in quads:
+        queue.dma_start(
+            out=plane[32 * quad : 32 * quad + 4, :].bitcast(I32),
+            in_=rows[0, 4 * quad : 4 * quad + 4, :].bitcast(I32),
+        )
+
+
+def tile_list_share_weighted_listed_rows_kernel(
+    tc, xt_words, xt_scales, wc_words, wc_scales, fj, wo_words, wo_scales, ws_words, ws_scales, offs, out
+):
+    nc = tc.nc
+    with ExitStack() as ctx:
+        keep = ctx.enter_context(tc.tile_pool(name="keep", bufs=1))
+        psum = ctx.enter_context(tc.psum_pool(name="psum", bufs=1))
+
+        offsets = keep.tile([P, J // 16], U16, name="offsets")
+        wc_w = keep.tile([P, C], U16, name="wc_w", align_bytes=64)
+        wc_s = keep.tile([P, C], U8, name="wc_s", align_bytes=64)
+        xt_w = keep.tile([P, T], U32, name="xt_w", align_bytes=64)
+        planes = keep.tile([P, T + N + N], U8, name="planes", align_bytes=64)
+        xt_s = planes[:, 0:T]
+        ws_s = planes[:, T : T + N]
+        wo_s = planes[:, T + N : T + N + N]
+        fj_col = keep.tile([P, 4], F32, name="fj_col")
+        fj_row = keep.tile([P, J], F32, name="fj_row")
+        ident = keep.tile([P, P], F32, name="ident")
+        got_w = keep.tile([P, J], U16, name="got_w", align_bytes=64)
+        got_s = keep.tile([P, J], U8, name="got_s", align_bytes=64)
+
+        nc.vector.memset(wc_s[:].bitcast(I32), 0)
+        nc.vector.memset(planes[:].bitcast(I32), 0)
+
+        ws_w = keep.tile([P, N], U16, name="ws_w", align_bytes=64)
+        wo_w = keep.tile([P, N], U32, name="wo_w", align_bytes=64)
+        nc.gpsimd.dma_start(out=fj_col[:], in_=fj.rearrange("(p i) o -> p (i o)", i=4))
+        make_identity(nc, ident[:])
+        load_scale_rows(nc.gpsimd, wo_s, wo_scales, range(0, 3))
+
+        nc.sync.dma_start(offsets[:], offs)
+        load_scale_rows(nc.sync, wc_s[:], wc_scales, range(0, 2))
+        load_scale_rows(nc.scalar, wc_s[:], wc_scales, range(2, 4))
+        nc.sync.dma_start(out=wc_w[:].bitcast(I32), in_=wc_words[0].bitcast(I32))
+        nc.sync.dma_start(out=xt_w[:].bitcast(I32), in_=xt_words[0].rearrange("p n r -> p (n r)").bitcast(I32))
+        load_scale_rows(nc.sync, ws_s, ws_scales, range(0, 2))
+        load_scale_rows(nc.sync, xt_s, xt_scales, range(4))
+        load_scale_rows(nc.sync, ws_s, ws_scales, range(2, 4))
+        nc.sync.dma_start(out=ws_w[:].bitcast(I32), in_=ws_words[0].bitcast(I32))
+        nc.sync.dma_start(out=wo_w[:].bitcast(I32), in_=wo_words[0].rearrange("p n r -> p (n r)").bitcast(I32))
+        load_scale_rows(nc.sync, wo_s, wo_scales, range(3, 4))
+
+        nc.vector.tensor_copy(got_s[:], wc_s[:].indirect(offsets[:]))
+        halves = [slice(0, J // 2), slice(J // 2, J)]
+        for h in range(2):
+            nc.vector.tensor_copy(got_w[:, halves[h]], wc_w[:].indirect(offsets[:, 16 * h : 16 * (h + 1)]))
+
+        z = {}
+
+        def scores(b):
+            z[b] = psum.tile([P, J], F32, name="z%d" % b, tag="z%d" % (b % 3))
+            cols = slice(b * P, (b + 1) * P)
+            for half in halves:
+                nc.tensor.matmul_mx(
+                    out=z[b][:, half], lhsT=xt_w[:, cols].bitcast(FP8X4), lhsT_scale=xt_s[:, cols],
+                    rhs=got_w[:, half].bitcast(FP4X4), rhs_scale=got_s[:, half], start=True, stop=True,
+                )
+
+        fj_ps = psum.tile([P, 4, P], F32, name="fj_ps", tag="spare")
+        for i in range(4):
+            nc.tensor.transpose(fj_ps[:, i, :], fj_col[:, i : i + 1].to_broadcast([P, P]), ident[:])
+        nc.scalar.activation(
+            out=fj_row[:].rearrange("p (u m e) -> p u m e", u=2, e=2),
+            in_=fj_ps[:].rearrange("p (u e) m -> p u m e", u=2),
+            func=ACT.Copy,
+        )
+
+        out_view = out.rearrange("(g p) t -> p g t", p=P)
+        e, inv, grouped, finished = {}, {}, {}, {}
+
+        def exponentiate(b):
+            scores(b)
+            neg_max = keep.tile([P, 1], F32, name="neg_max%d" % b)
+            nc.vector.tensor_reduce(out=neg_max[:], in_=z[b][:], axis=AXIS.X, op=ALU.max, negate=True)
+            e[b] = keep.tile([P, J], F32, name="e%d" % b)
+            total = keep.tile([P, 1], F32, name="total%d" % b)
+            nc.scalar.activation(
+                out=e[b][:].rearrange("p (u m e) -> p u m e", u=2, e=2),
+                in_=z[b][:].rearrange("p (m u e) -> p u m e", u=2, e=2),
+                func=ACT.Exp, bias=neg_max[:], accum_out=total[:],
+            )
+            inv[b] = keep.tile([P, 1], F32, name="inv%d" % b)
+            nc.vector.reciprocal(out=inv[b][:], in_=total[:])
+
+        def weigh_and_turn(b):
+            qw = keep.tile([P, J], BF16, name="qw%d" % b, align_bytes=64)
+            nc.vector.scalar_tensor_tensor(
+                out=qw[:], in0=e[b][:], scalar=inv[b][:], in1=fj_row[:], op0=ALU.mult, op1=ALU.mult
+            )
+            turned = psum.tile([P, 2, P], F32, name="turned%d" % b, tag=("spare" if b == 0 else "z%d" % (b % 3)))
+            pairs = qw[:].bitcast(F32)
+            for u in range(2):
+                nc.tensor.transpose(turned[:, u, :], pairs[:, u * P : (u + 1) * P], ident[:])
+            grouped[b] = keep.tile([P, 4 * P], BF16, name="grouped%d" % b, align_bytes=64)
+            nc.scalar.copy(
+                out=grouped[b][:].bitcast(F32).rearrange("p (t u) -> p t u", u=2),
+                in_=turned[:].rearrange("p u t -> p t u"),
+            )
+
+        def skip_product(bank, b, groups):
+            cols = slice(b * P, (b + 1) * P)
+            for place, g in enumerate(groups):
+                rows = slice(g * P, (g + 1) * P)
+                nc.tensor.matmul_mx(
+                    out=bank[:, place, :], lhsT=ws_w[:, rows].bitcast(FP4X4), lhsT_scale=ws_s[:, rows],
+                    rhs=xt_w[:, cols].bitcast(FP8X4), rhs_scale=xt_s[:, cols], start=(place == 0), stop=False,
+                )
+
+        def finish(b):
+            parts = [(range(0, 4), "out%d" % b, nc.scalar.copy, nc.sync)]
+            if b == BLOCKS - 1:
+                parts = [(range(0, 2), "out%d" % b, nc.scalar.copy, nc.sync), (range(2, 4), "spare", nc.vector.tensor_copy, nc.scalar)]
+            banks = []
+            for groups, tag, copy, queue in parts:
+                bank = psum.tile([P, len(groups), P], F32, name="acc%d_%d" % (b, groups[0]), tag=tag)
+                skip_product(bank, b, groups)
+                banks.append(bank)
+            q_w = keep.tile([P, P], U32, name="q_w%d" % b, align_bytes=64)
+            q_s = keep.tile([P, P], U8, name="q_s%d" % b, align_bytes=64)
+            nc.vector.quantize_mx(out=q_w[:].bitcast(FP8X4), scales=q_s[:], in_=grouped[b][:])
+            for bank, (groups, tag, copy, queue) in zip(banks, parts):
+                for place, g in enumerate(groups):
+                    rows = slice(g * P, (g + 1) * P)
+                    nc.tensor.matmul_mx(
+                        out=bank[:, place, :], lhsT=wo_w[:, rows].bitcast(FP8X4), lhsT_scale=wo_s[:, rows],
+                        rhs=q_w[:].bitcast(FP8X4), rhs_scale=q_s[:], start=False, stop=(place == len(groups) - 1),
+                    )
+            finished[b] = (banks, parts)
+
+        def store(b):
+            banks, parts = finished[b]
+            for bank, (groups, tag, copy, queue) in zip(banks, parts):
+                res = keep.tile([P, len(groups), P], F32, name="res%d_%d" % (b, groups[0]))
+                copy(out=res[:], in_=bank[:])
+                queue.dma_start(out=out_view[:, groups[0] : groups[-1] + 1, b * P : (b + 1) * P], in_=res[:])
+
+        for step in range(BLOCKS + 3):
+            if step < BLOCKS:
+                exponentiate(step)
+            if 1 <= step <= BLOCKS:
+                weigh_and_turn(step - 1)
+            if 2 <= step <= BLOCKS + 1:
+                finish(step - 2)
+            if step >= 3:
+                store(step - 3)

@@ -1,7 +1,6 @@
 from contextlib import ExitStack
 
 import concourse.mybir as mybir
-from concourse.masks import make_identity
 
 K, T, C, J, N = 512, 512, 2048, 512, 512
 FLOPS = 2 * K * T * J + 2 * J * N * T + 2 * K * N * T
@@ -39,7 +38,7 @@ def tile_list_share_weighted_listed_rows_kernel(
         psum = ctx.enter_context(tc.psum_pool(name="psum", bufs=1))
 
         offsets = keep.tile([P, J // 16], U16, name="offsets")
-        wc_w = keep.tile([P, C], U16, name="wc_w", align_bytes=64)
+        wc_w = keep.tile([P, C], U16, name="wc_w", tag="table", align_bytes=64)
         wc_s = keep.tile([P, C], U8, name="wc_s", align_bytes=64)
         xt_w = keep.tile([P, T], U32, name="xt_w", align_bytes=64)
         planes = keep.tile([P, T + N + N], U8, name="planes", align_bytes=64)
@@ -47,7 +46,6 @@ def tile_list_share_weighted_listed_rows_kernel(
         ws_s = planes[:, T : T + N]
         wo_s = planes[:, T + N : T + N + N]
         fj_col = keep.tile([P, 4], F32, name="fj_col")
-        fj_row = keep.tile([P, J], F32, name="fj_row")
         ident = keep.tile([P, P], F32, name="ident")
         got_w = keep.tile([P, J], U16, name="got_w", align_bytes=64)
         got_s = keep.tile([P, J], U8, name="got_s", align_bytes=64)
@@ -57,21 +55,36 @@ def tile_list_share_weighted_listed_rows_kernel(
 
         ws_w = keep.tile([P, N], U16, name="ws_w", align_bytes=64)
         wo_w = keep.tile([P, N], U32, name="wo_w", align_bytes=64)
+        ones = keep.tile([P, P], F32, name="ones")
+        column = keep.tile([P, P], F32, name="column", align_bytes=64)
+        in_quadrant = keep.tile([P, 32], F32, name="in_quadrant", align_bytes=64)
+        quadrant_start = keep.tile([P, 1], F32, name="quadrant_start")
+        nc.gpsimd.memset(ones[:], 1.0)
         nc.gpsimd.dma_start(out=fj_col[:], in_=fj.rearrange("(p i) o -> p (i o)", i=4))
-        make_identity(nc, ident[:])
-        load_scale_rows(nc.gpsimd, wo_s, wo_scales, range(0, 3))
+        for quad in range(4):
+            nc.vector.memset(quadrant_start[32 * quad : 32 * (quad + 1), :], float(32 * quad))
+        nc.vector.tensor_tensor_scan(
+            out=column[:], data0=ones[:], data1=ones[:], initial=-1.0, op0=ALU.mult, op1=ALU.add
+        )
+        nc.vector.transpose(out=in_quadrant[:], in_=column[:, 0:32])
+        nc.vector.tensor_scalar(
+            out=ident[:], in0=column[:], scalar1=quadrant_start[:], scalar2=in_quadrant[:, 0:1],
+            op0=ALU.subtract, op1=ALU.is_equal,
+        )
 
         nc.sync.dma_start(offsets[:], offs)
+        nc.sync.dma_start(out=xt_w[:].bitcast(I32), in_=xt_words[0].rearrange("p n r -> p (n r)").bitcast(I32))
         load_scale_rows(nc.sync, wc_s[:], wc_scales, range(0, 2))
         load_scale_rows(nc.scalar, wc_s[:], wc_scales, range(2, 4))
         nc.sync.dma_start(out=wc_w[:].bitcast(I32), in_=wc_words[0].bitcast(I32))
-        nc.sync.dma_start(out=xt_w[:].bitcast(I32), in_=xt_words[0].rearrange("p n r -> p (n r)").bitcast(I32))
-        load_scale_rows(nc.sync, ws_s, ws_scales, range(0, 2))
-        load_scale_rows(nc.sync, xt_s, xt_scales, range(4))
-        load_scale_rows(nc.sync, ws_s, ws_scales, range(2, 4))
+        load_scale_rows(nc.scalar, xt_s, xt_scales, range(0, 3))
+        load_scale_rows(nc.sync, xt_s, xt_scales, range(3, 4))
         nc.sync.dma_start(out=ws_w[:].bitcast(I32), in_=ws_words[0].bitcast(I32))
+        load_scale_rows(nc.scalar, ws_s, ws_scales, range(0, 2))
+        load_scale_rows(nc.sync, ws_s, ws_scales, range(2, 4))
         nc.sync.dma_start(out=wo_w[:].bitcast(I32), in_=wo_words[0].rearrange("p n r -> p (n r)").bitcast(I32))
-        load_scale_rows(nc.sync, wo_s, wo_scales, range(3, 4))
+        load_scale_rows(nc.scalar, wo_s, wo_scales, range(0, 2))
+        load_scale_rows(nc.sync, wo_s, wo_scales, range(2, 4))
 
         nc.vector.tensor_copy(got_s[:], wc_s[:].indirect(offsets[:]))
         halves = [slice(0, J // 2), slice(J // 2, J)]
@@ -81,7 +94,7 @@ def tile_list_share_weighted_listed_rows_kernel(
         z = {}
 
         def scores(b):
-            z[b] = psum.tile([P, J], F32, name="z%d" % b, tag="z%d" % (b % 3))
+            z[b] = psum.tile([P, J], F32, name="z%d" % b, tag="z%d" % (b % 2))
             cols = slice(b * P, (b + 1) * P)
             for half in halves:
                 nc.tensor.matmul_mx(
@@ -89,13 +102,13 @@ def tile_list_share_weighted_listed_rows_kernel(
                     rhs=got_w[:, half].bitcast(FP4X4), rhs_scale=got_s[:, half], start=True, stop=True,
                 )
 
-        fj_ps = psum.tile([P, 4, P], F32, name="fj_ps", tag="spare")
+        fj_ps = psum.tile([P, 4, P], F32, name="fj_ps", tag="bank1")
         for i in range(4):
             nc.tensor.transpose(fj_ps[:, i, :], fj_col[:, i : i + 1].to_broadcast([P, P]), ident[:])
-        nc.scalar.activation(
+        fj_row = keep.tile([P, J], F32, name="fj_row", tag="table", align_bytes=64)
+        nc.vector.tensor_copy(
             out=fj_row[:].rearrange("p (u m e) -> p u m e", u=2, e=2),
             in_=fj_ps[:].rearrange("p (u e) m -> p u m e", u=2),
-            func=ACT.Copy,
         )
 
         out_view = out.rearrange("(g p) t -> p g t", p=P)
@@ -120,7 +133,7 @@ def tile_list_share_weighted_listed_rows_kernel(
             nc.vector.scalar_tensor_tensor(
                 out=qw[:], in0=e[b][:], scalar=inv[b][:], in1=fj_row[:], op0=ALU.mult, op1=ALU.mult
             )
-            turned = psum.tile([P, 2, P], F32, name="turned%d" % b, tag=("spare" if b == 0 else "z%d" % (b % 3)))
+            turned = psum.tile([P, 2, P], F32, name="turned%d" % b, tag="bank%d" % (b + 1))
             pairs = qw[:].bitcast(F32)
             for u in range(2):
                 nc.tensor.transpose(turned[:, u, :], pairs[:, u * P : (u + 1) * P], ident[:])
@@ -140,9 +153,9 @@ def tile_list_share_weighted_listed_rows_kernel(
                 )
 
         def finish(b):
-            parts = [(range(0, 4), "out%d" % b, nc.scalar.copy, nc.sync)]
+            parts = [(range(0, 4), "bank%d" % b, nc.scalar.copy, nc.sync)]
             if b == BLOCKS - 1:
-                parts = [(range(0, 2), "out%d" % b, nc.scalar.copy, nc.sync), (range(2, 4), "spare", nc.vector.tensor_copy, nc.scalar)]
+                parts = [(range(0, 2), "bank%d" % b, nc.scalar.copy, nc.sync), (range(2, 4), "z0", nc.vector.tensor_copy, nc.scalar)]
             banks = []
             for groups, tag, copy, queue in parts:
                 bank = psum.tile([P, len(groups), P], F32, name="acc%d_%d" % (b, groups[0]), tag=tag)

@@ -83,7 +83,7 @@ def tile_list_share_weighted_listed_rows_kernel(
         load_scale_rows(nc.scalar, ws_s, ws_scales, range(0, 2))
         load_scale_rows(nc.sync, ws_s, ws_scales, range(2, 4))
         nc.sync.dma_start(out=wo_w[:].bitcast(I32), in_=wo_words[0].rearrange("p n r -> p (n r)").bitcast(I32))
-        load_scale_rows(nc.scalar, wo_s, wo_scales, range(0, 2))
+        load_scale_rows(nc.gpsimd, wo_s, wo_scales, range(0, 2))
         load_scale_rows(nc.sync, wo_s, wo_scales, range(2, 4))
 
         nc.vector.tensor_copy(got_s[:], wc_s[:].indirect(offsets[:]))
@@ -94,7 +94,7 @@ def tile_list_share_weighted_listed_rows_kernel(
         z = {}
 
         def scores(b):
-            z[b] = psum.tile([P, J], F32, name="z%d" % b, tag="z%d" % (b % 2))
+            z[b] = psum.tile([P, J], F32, name="z%d" % b, tag="z%d" % (b % 3))
             cols = slice(b * P, (b + 1) * P)
             for half in halves:
                 nc.tensor.matmul_mx(
@@ -102,7 +102,7 @@ def tile_list_share_weighted_listed_rows_kernel(
                     rhs=got_w[:, half].bitcast(FP4X4), rhs_scale=got_s[:, half], start=True, stop=True,
                 )
 
-        fj_ps = psum.tile([P, 4, P], F32, name="fj_ps", tag="bank1")
+        fj_ps = psum.tile([P, 4, P], F32, name="fj_ps", tag="bank2")
         for i in range(4):
             nc.tensor.transpose(fj_ps[:, i, :], fj_col[:, i : i + 1].to_broadcast([P, P]), ident[:])
         fj_row = keep.tile([P, J], F32, name="fj_row", tag="table", align_bytes=64)
@@ -118,7 +118,7 @@ def tile_list_share_weighted_listed_rows_kernel(
             scores(b)
             neg_max = keep.tile([P, 1], F32, name="neg_max%d" % b)
             nc.vector.tensor_reduce(out=neg_max[:], in_=z[b][:], axis=AXIS.X, op=ALU.max, negate=True)
-            e[b] = keep.tile([P, J], F32, name="e%d" % b)
+            e[b] = keep.tile([P, J], F32, name="e%d" % b, tag="wide%d" % b, align_bytes=64)
             total = keep.tile([P, 1], F32, name="total%d" % b)
             nc.scalar.activation(
                 out=e[b][:].rearrange("p (u m e) -> p u m e", u=2, e=2),
@@ -129,11 +129,11 @@ def tile_list_share_weighted_listed_rows_kernel(
             nc.vector.reciprocal(out=inv[b][:], in_=total[:])
 
         def weigh_and_turn(b):
-            qw = keep.tile([P, J], BF16, name="qw%d" % b, align_bytes=64)
+            qw = keep.tile([P, J], BF16, name="qw%d" % b, tag="wide%d" % (b + 3), align_bytes=64)
             nc.vector.scalar_tensor_tensor(
                 out=qw[:], in0=e[b][:], scalar=inv[b][:], in1=fj_row[:], op0=ALU.mult, op1=ALU.mult
             )
-            turned = psum.tile([P, 2, P], F32, name="turned%d" % b, tag="bank%d" % (b + 1))
+            turned = psum.tile([P, 2, P], F32, name="turned%d" % b, tag=("bank2", "z1", "bank3", "z0")[b])
             pairs = qw[:].bitcast(F32)
             for u in range(2):
                 nc.tensor.transpose(turned[:, u, :], pairs[:, u * P : (u + 1) * P], ident[:])
@@ -155,7 +155,7 @@ def tile_list_share_weighted_listed_rows_kernel(
         def finish(b):
             parts = [(range(0, 4), "bank%d" % b, nc.scalar.copy, nc.sync)]
             if b == BLOCKS - 1:
-                parts = [(range(0, 2), "bank%d" % b, nc.scalar.copy, nc.sync), (range(2, 4), "z0", nc.vector.tensor_copy, nc.scalar)]
+                parts = [(range(0, 2), "z1", nc.scalar.copy, nc.sync), (range(2, 4), "z2", nc.vector.tensor_copy, nc.scalar)]
             banks = []
             for groups, tag, copy, queue in parts:
                 bank = psum.tile([P, len(groups), P], F32, name="acc%d_%d" % (b, groups[0]), tag=tag)

@@ -18,14 +18,23 @@ ALU = mybir.AluOpType
 AXIS = mybir.AxisListType
 
 P = 128
-BLOCKS = T // P
+PACK = 4
+QUADRANT = 32
+QUADRANTS = P // QUADRANT
+ENTRIES_PER_COLUMN = 16
+TOKEN_BLOCKS = T // P
+MX_ALIGN = 64
+
+SCORE_BANKS = ("score0", "score1", "score2", "score0")
+TURN_BANKS = ("shared", "score1", "turn2", "score0")
+FACTOR_BANK = "shared"
 
 
-def load_scale_rows(queue, plane, rows, quads):
-    for quad in quads:
+def load_scale_rows(queue, plane, rows, quadrants):
+    for q in quadrants:
         queue.dma_start(
-            out=plane[32 * quad : 32 * quad + 4, :].bitcast(I32),
-            in_=rows[0, 4 * quad : 4 * quad + 4, :].bitcast(I32),
+            out=plane[QUADRANT * q : QUADRANT * q + 4, :].bitcast(I32),
+            in_=rows[0, 4 * q : 4 * q + 4, :].bitcast(I32),
         )
 
 
@@ -37,36 +46,37 @@ def tile_list_share_weighted_listed_rows_kernel(
         keep = ctx.enter_context(tc.tile_pool(name="keep", bufs=1))
         psum = ctx.enter_context(tc.psum_pool(name="psum", bufs=1))
 
-        offsets = keep.tile([P, J // 16], U16, name="offsets")
-        wc_w = keep.tile([P, C], U16, name="wc_w", tag="table", align_bytes=64)
-        wc_s = keep.tile([P, C], U8, name="wc_s", align_bytes=64)
-        xt_w = keep.tile([P, T], U32, name="xt_w", align_bytes=64)
-        planes = keep.tile([P, T + N + N], U8, name="planes", align_bytes=64)
+        offsets = keep.tile([P, J // ENTRIES_PER_COLUMN], U16, name="offsets")
+        wc_w = keep.tile([P, C], U16, name="wc_w", tag="table", align_bytes=MX_ALIGN)
+        wc_s = keep.tile([P, C], U8, name="wc_s", align_bytes=MX_ALIGN)
+        xt_w = keep.tile([P, T], U32, name="xt_w", align_bytes=MX_ALIGN)
+        planes = keep.tile([P, T + N + N], U8, name="planes", align_bytes=MX_ALIGN)
         xt_s = planes[:, 0:T]
         ws_s = planes[:, T : T + N]
         wo_s = planes[:, T + N : T + N + N]
-        fj_col = keep.tile([P, 4], F32, name="fj_col")
+        fj_col = keep.tile([P, PACK], F32, name="fj_col")
         ident = keep.tile([P, P], F32, name="ident")
-        got_w = keep.tile([P, J], U16, name="got_w", align_bytes=64)
-        got_s = keep.tile([P, J], U8, name="got_s", align_bytes=64)
+        got_w = keep.tile([P, J], U16, name="got_w", align_bytes=MX_ALIGN)
+        got_s = keep.tile([P, J], U8, name="got_s", align_bytes=MX_ALIGN)
 
         nc.vector.memset(wc_s[:].bitcast(I32), 0)
         nc.vector.memset(planes[:].bitcast(I32), 0)
 
-        ws_w = keep.tile([P, N], U16, name="ws_w", align_bytes=64)
-        wo_w = keep.tile([P, N], U32, name="wo_w", align_bytes=64)
+        ws_w = keep.tile([P, N], U16, name="ws_w", align_bytes=MX_ALIGN)
+        wo_w = keep.tile([P, N], U32, name="wo_w", align_bytes=MX_ALIGN)
+
         ones = keep.tile([P, P], F32, name="ones")
-        column = keep.tile([P, P], F32, name="column", align_bytes=64)
-        in_quadrant = keep.tile([P, 32], F32, name="in_quadrant", align_bytes=64)
+        column = keep.tile([P, P], F32, name="column", align_bytes=MX_ALIGN)
+        in_quadrant = keep.tile([P, QUADRANT], F32, name="in_quadrant", align_bytes=MX_ALIGN)
         quadrant_start = keep.tile([P, 1], F32, name="quadrant_start")
         nc.gpsimd.memset(ones[:], 1.0)
-        nc.gpsimd.dma_start(out=fj_col[:], in_=fj.rearrange("(p i) o -> p (i o)", i=4))
-        for quad in range(4):
-            nc.vector.memset(quadrant_start[32 * quad : 32 * (quad + 1), :], float(32 * quad))
+        nc.gpsimd.dma_start(out=fj_col[:], in_=fj.rearrange("(p i) o -> p (i o)", i=PACK))
+        for q in range(QUADRANTS):
+            nc.vector.memset(quadrant_start[QUADRANT * q : QUADRANT * (q + 1), :], float(QUADRANT * q))
         nc.vector.tensor_tensor_scan(
             out=column[:], data0=ones[:], data1=ones[:], initial=-1.0, op0=ALU.mult, op1=ALU.add
         )
-        nc.vector.transpose(out=in_quadrant[:], in_=column[:, 0:32])
+        nc.vector.transpose(out=in_quadrant[:], in_=column[:, 0:QUADRANT])
         nc.vector.tensor_scalar(
             out=ident[:], in0=column[:], scalar1=quadrant_start[:], scalar2=in_quadrant[:, 0:1],
             op0=ALU.subtract, op1=ALU.is_equal,
@@ -88,104 +98,96 @@ def tile_list_share_weighted_listed_rows_kernel(
 
         nc.vector.tensor_copy(got_s[:], wc_s[:].indirect(offsets[:]))
         halves = [slice(0, J // 2), slice(J // 2, J)]
-        for h in range(2):
-            nc.vector.tensor_copy(got_w[:, halves[h]], wc_w[:].indirect(offsets[:, 16 * h : 16 * (h + 1)]))
+        for half in halves:
+            list_columns = slice(half.start // ENTRIES_PER_COLUMN, half.stop // ENTRIES_PER_COLUMN)
+            nc.vector.tensor_copy(got_w[:, half], wc_w[:].indirect(offsets[:, list_columns]))
 
-        z = {}
-
-        def scores(b):
-            z[b] = psum.tile([P, J], F32, name="z%d" % b, tag="z%d" % (b % 3))
-            cols = slice(b * P, (b + 1) * P)
-            for half in halves:
-                nc.tensor.matmul_mx(
-                    out=z[b][:, half], lhsT=xt_w[:, cols].bitcast(FP8X4), lhsT_scale=xt_s[:, cols],
-                    rhs=got_w[:, half].bitcast(FP4X4), rhs_scale=got_s[:, half], start=True, stop=True,
-                )
-
-        fj_ps = psum.tile([P, 4, P], F32, name="fj_ps", tag="bank2")
-        for i in range(4):
-            nc.tensor.transpose(fj_ps[:, i, :], fj_col[:, i : i + 1].to_broadcast([P, P]), ident[:])
-        fj_row = keep.tile([P, J], F32, name="fj_row", tag="table", align_bytes=64)
+        fj_turned = psum.tile([P, PACK, P], F32, name="fj_turned", tag=FACTOR_BANK)
+        for i in range(PACK):
+            nc.tensor.transpose(fj_turned[:, i, :], fj_col[:, i : i + 1].to_broadcast([P, P]), ident[:])
+        fj_row = keep.tile([P, J], F32, name="fj_row", tag="table", align_bytes=MX_ALIGN)
         nc.vector.tensor_copy(
             out=fj_row[:].rearrange("p (u m e) -> p u m e", u=2, e=2),
-            in_=fj_ps[:].rearrange("p (u e) m -> p u m e", u=2),
+            in_=fj_turned[:].rearrange("p (u e) m -> p u m e", u=2),
         )
 
+        result_parts = (
+            [(range(0, 4), "result0", nc.scalar.copy, nc.sync)],
+            [(range(0, 4), "result1", nc.vector.tensor_copy, nc.sync)],
+            [(range(0, 2), "shared", nc.scalar.copy, nc.sync), (range(2, 4), "score2", nc.scalar.copy, nc.sync)],
+            [(range(0, 2), "score1", nc.scalar.copy, nc.sync), (range(2, 4), "result3", nc.vector.tensor_copy, nc.scalar)],
+        )
         out_view = out.rearrange("(g p) t -> p g t", p=P)
-        e, inv, grouped, finished = {}, {}, {}, {}
+        exps, inverse_sums, interleaved, result_banks = {}, {}, {}, {}
 
         def exponentiate(b):
-            scores(b)
+            scores = psum.tile([P, J], F32, name="scores%d" % b, tag=SCORE_BANKS[b])
+            tokens = slice(b * P, (b + 1) * P)
+            for half in halves:
+                nc.tensor.matmul_mx(
+                    out=scores[:, half], lhsT=xt_w[:, tokens].bitcast(FP8X4), lhsT_scale=xt_s[:, tokens],
+                    rhs=got_w[:, half].bitcast(FP4X4), rhs_scale=got_s[:, half], start=True, stop=True,
+                )
             neg_max = keep.tile([P, 1], F32, name="neg_max%d" % b)
-            nc.vector.tensor_reduce(out=neg_max[:], in_=z[b][:], axis=AXIS.X, op=ALU.max, negate=True)
-            e[b] = keep.tile([P, J], F32, name="e%d" % b, tag="wide%d" % b, align_bytes=64)
+            nc.vector.tensor_reduce(out=neg_max[:], in_=scores[:], axis=AXIS.X, op=ALU.max, negate=True)
+            exps[b] = keep.tile([P, J], F32, name="exps%d" % b, tag="wide%d" % b, align_bytes=MX_ALIGN)
             total = keep.tile([P, 1], F32, name="total%d" % b)
             nc.scalar.activation(
-                out=e[b][:].rearrange("p (u m e) -> p u m e", u=2, e=2),
-                in_=z[b][:].rearrange("p (m u e) -> p u m e", u=2, e=2),
+                out=exps[b][:].rearrange("p (u m e) -> p u m e", u=2, e=2),
+                in_=scores[:].rearrange("p (m u e) -> p u m e", u=2, e=2),
                 func=ACT.Exp, bias=neg_max[:], accum_out=total[:],
             )
-            inv[b] = keep.tile([P, 1], F32, name="inv%d" % b)
-            nc.vector.reciprocal(out=inv[b][:], in_=total[:])
+            inverse_sums[b] = keep.tile([P, 1], F32, name="inverse_sum%d" % b)
+            nc.vector.reciprocal(out=inverse_sums[b][:], in_=total[:])
 
         def weigh_and_turn(b):
-            qw = keep.tile([P, J], BF16, name="qw%d" % b, tag="wide%d" % (b + 3), align_bytes=64)
+            qw = keep.tile([P, J], BF16, name="qw%d" % b, tag="wide%d" % (b + TOKEN_BLOCKS - 1), align_bytes=MX_ALIGN)
             nc.vector.scalar_tensor_tensor(
-                out=qw[:], in0=e[b][:], scalar=inv[b][:], in1=fj_row[:], op0=ALU.mult, op1=ALU.mult
+                out=qw[:], in0=exps[b][:], scalar=inverse_sums[b][:], in1=fj_row[:], op0=ALU.mult, op1=ALU.mult
             )
-            turned = psum.tile([P, 2, P], F32, name="turned%d" % b, tag=("bank2", "z1", "bank3", "z0")[b])
+            turned = psum.tile([P, 2, P], F32, name="turned%d" % b, tag=TURN_BANKS[b])
             pairs = qw[:].bitcast(F32)
             for u in range(2):
                 nc.tensor.transpose(turned[:, u, :], pairs[:, u * P : (u + 1) * P], ident[:])
-            grouped[b] = keep.tile([P, 4 * P], BF16, name="grouped%d" % b, align_bytes=64)
+            interleaved[b] = keep.tile([P, PACK * P], BF16, name="interleaved%d" % b, align_bytes=MX_ALIGN)
             nc.scalar.copy(
-                out=grouped[b][:].bitcast(F32).rearrange("p (t u) -> p t u", u=2),
+                out=interleaved[b][:].bitcast(F32).rearrange("p (t u) -> p t u", u=2),
                 in_=turned[:].rearrange("p u t -> p t u"),
             )
 
-        def skip_product(bank, b, groups):
-            cols = slice(b * P, (b + 1) * P)
-            for place, g in enumerate(groups):
-                rows = slice(g * P, (g + 1) * P)
-                nc.tensor.matmul_mx(
-                    out=bank[:, place, :], lhsT=ws_w[:, rows].bitcast(FP4X4), lhsT_scale=ws_s[:, rows],
-                    rhs=xt_w[:, cols].bitcast(FP8X4), rhs_scale=xt_s[:, cols], start=(place == 0), stop=False,
-                )
-
-        def finish(b):
-            parts = [(range(0, 4), "bank%d" % b, nc.scalar.copy, nc.sync)]
-            if b == BLOCKS - 1:
-                parts = [(range(0, 2), "z1", nc.scalar.copy, nc.sync), (range(2, 4), "z2", nc.vector.tensor_copy, nc.scalar)]
-            banks = []
-            for groups, tag, copy, queue in parts:
-                bank = psum.tile([P, len(groups), P], F32, name="acc%d_%d" % (b, groups[0]), tag=tag)
-                skip_product(bank, b, groups)
-                banks.append(bank)
-            q_w = keep.tile([P, P], U32, name="q_w%d" % b, align_bytes=64)
-            q_s = keep.tile([P, P], U8, name="q_s%d" % b, align_bytes=64)
-            nc.vector.quantize_mx(out=q_w[:].bitcast(FP8X4), scales=q_s[:], in_=grouped[b][:])
-            for bank, (groups, tag, copy, queue) in zip(banks, parts):
+        def multiply(b):
+            tokens = slice(b * P, (b + 1) * P)
+            result_banks[b] = []
+            for groups, tag, copy, queue in result_parts[b]:
+                bank = psum.tile([P, len(groups), P], F32, name="result%d_%d" % (b, groups[0]), tag=tag)
+                for place, g in enumerate(groups):
+                    rows = slice(g * P, (g + 1) * P)
+                    nc.tensor.matmul_mx(
+                        out=bank[:, place, :], lhsT=ws_w[:, rows].bitcast(FP4X4), lhsT_scale=ws_s[:, rows],
+                        rhs=xt_w[:, tokens].bitcast(FP8X4), rhs_scale=xt_s[:, tokens],
+                        start=(place == 0), stop=False,
+                    )
+                result_banks[b].append(bank)
+            qw_w = keep.tile([P, P], U32, name="qw_w%d" % b, align_bytes=MX_ALIGN)
+            qw_s = keep.tile([P, P], U8, name="qw_s%d" % b, align_bytes=MX_ALIGN)
+            nc.vector.quantize_mx(out=qw_w[:].bitcast(FP8X4), scales=qw_s[:], in_=interleaved[b][:])
+            for bank, (groups, tag, copy, queue) in zip(result_banks[b], result_parts[b]):
                 for place, g in enumerate(groups):
                     rows = slice(g * P, (g + 1) * P)
                     nc.tensor.matmul_mx(
                         out=bank[:, place, :], lhsT=wo_w[:, rows].bitcast(FP8X4), lhsT_scale=wo_s[:, rows],
-                        rhs=q_w[:].bitcast(FP8X4), rhs_scale=q_s[:], start=False, stop=(place == len(groups) - 1),
+                        rhs=qw_w[:].bitcast(FP8X4), rhs_scale=qw_s[:],
+                        start=False, stop=(place == len(groups) - 1),
                     )
-            finished[b] = (banks, parts)
 
         def store(b):
-            banks, parts = finished[b]
-            for bank, (groups, tag, copy, queue) in zip(banks, parts):
-                res = keep.tile([P, len(groups), P], F32, name="res%d_%d" % (b, groups[0]))
-                copy(out=res[:], in_=bank[:])
-                queue.dma_start(out=out_view[:, groups[0] : groups[-1] + 1, b * P : (b + 1) * P], in_=res[:])
+            for bank, (groups, tag, copy, queue) in zip(result_banks[b], result_parts[b]):
+                staged = keep.tile([P, len(groups), P], F32, name="staged%d_%d" % (b, groups[0]))
+                copy(out=staged[:], in_=bank[:])
+                queue.dma_start(out=out_view[:, groups[0] : groups[-1] + 1, b * P : (b + 1) * P], in_=staged[:])
 
-        for step in range(BLOCKS + 3):
-            if step < BLOCKS:
-                exponentiate(step)
-            if 1 <= step <= BLOCKS:
-                weigh_and_turn(step - 1)
-            if 2 <= step <= BLOCKS + 1:
-                finish(step - 2)
-            if step >= 3:
-                store(step - 3)
+        stages = (exponentiate, weigh_and_turn, multiply, store)
+        for step in range(TOKEN_BLOCKS + len(stages) - 1):
+            for lag, stage in enumerate(stages):
+                if 0 <= step - lag < TOKEN_BLOCKS:
+                    stage(step - lag)

@@ -69,8 +69,8 @@ def tile_list_share_weighted_listed_rows_kernel(
         column = keep.tile([P, P], F32, name="column", align_bytes=MX_ALIGN)
         in_quadrant = keep.tile([P, QUADRANT], F32, name="in_quadrant", align_bytes=MX_ALIGN)
         quadrant_start = keep.tile([P, 1], F32, name="quadrant_start")
-        nc.gpsimd.memset(ones[:], 1.0)
         nc.gpsimd.dma_start(out=fj_col[:], in_=fj.rearrange("(p i) o -> p (i o)", i=PACK))
+        nc.vector.memset(ones[:], 1.0)
         for q in range(QUADRANTS):
             nc.vector.memset(quadrant_start[QUADRANT * q : QUADRANT * (q + 1), :], float(QUADRANT * q))
         nc.vector.tensor_tensor_scan(

from contextlib import ExitStack

import concourse.mybir as mybir

K, T, C, J, N = 512, 512, 2048, 512, 512
FLOPS = 2 * K * T * J + 2 * J * N * T + 2 * K * N * T

F32 = mybir.dt.float32
BF16 = mybir.dt.bfloat16
I32 = mybir.dt.int32
U32 = mybir.dt.uint32
U16 = mybir.dt.uint16
U8 = mybir.dt.uint8
FP8X4 = mybir.dt.float8_e4m3fn_x4
FP4X4 = mybir.dt.float4_e2m1fn_x4
ACT = mybir.ActivationFunctionType
ALU = mybir.AluOpType
AXIS = mybir.AxisListType

P = 128
PACK = 4
QUADRANT = 32
QUADRANTS = P // QUADRANT
ENTRIES_PER_COLUMN = 16
TOKEN_BLOCKS = T // P
MX_ALIGN = 64

SCORE_BANKS = ("score0", "score1", "score2", "score0")
TURN_BANKS = ("shared", "score1", "turn2", "score0")
FACTOR_BANK = "shared"


def load_scale_rows(queue, plane, rows, quadrants):
    for q in quadrants:
        queue.dma_start(
            out=plane[QUADRANT * q : QUADRANT * q + 4, :].bitcast(I32),
            in_=rows[0, 4 * q : 4 * q + 4, :].bitcast(I32),
        )


def tile_list_share_weighted_listed_rows_kernel(
    tc, xt_words, xt_scales, wc_words, wc_scales, fj, wo_words, wo_scales, ws_words, ws_scales, offs, out
):
    nc = tc.nc
    with ExitStack() as ctx:
        keep = ctx.enter_context(tc.tile_pool(name="keep", bufs=1))
        psum = ctx.enter_context(tc.psum_pool(name="psum", bufs=1))

        offsets = keep.tile([P, J // ENTRIES_PER_COLUMN], U16, name="offsets")
        wc_w = keep.tile([P, C], U16, name="wc_w", tag="table", align_bytes=MX_ALIGN)
        wc_s = keep.tile([P, C], U8, name="wc_s", align_bytes=MX_ALIGN)
        xt_w = keep.tile([P, T], U32, name="xt_w", align_bytes=MX_ALIGN)
        planes = keep.tile([P, T + N + N], U8, name="planes", align_bytes=MX_ALIGN)
        xt_s = planes[:, 0:T]
        ws_s = planes[:, T : T + N]
        wo_s = planes[:, T + N : T + N + N]
        fj_col = keep.tile([P, PACK], F32, name="fj_col")
        ident = keep.tile([P, P], F32, name="ident")
        got_w = keep.tile([P, J], U16, name="got_w", align_bytes=MX_ALIGN)
        got_s = keep.tile([P, J], U8, name="got_s", align_bytes=MX_ALIGN)

        nc.vector.memset(wc_s[:].bitcast(I32), 0)
        nc.vector.memset(planes[:].bitcast(I32), 0)

        ws_w = keep.tile([P, N], U16, name="ws_w", align_bytes=MX_ALIGN)
        wo_w = keep.tile([P, N], U32, name="wo_w", align_bytes=MX_ALIGN)

        ones = keep.tile([P, P], F32, name="ones")
        column = keep.tile([P, P], F32, name="column", align_bytes=MX_ALIGN)
        in_quadrant = keep.tile([P, QUADRANT], F32, name="in_quadrant", align_bytes=MX_ALIGN)
        quadrant_start = keep.tile([P, 1], F32, name="quadrant_start")
        nc.gpsimd.dma_start(out=fj_col[:], in_=fj.rearrange("(p i) o -> p (i o)", i=PACK))
        nc.vector.memset(ones[:], 1.0)
        for q in range(QUADRANTS):
            nc.vector.memset(quadrant_start[QUADRANT * q : QUADRANT * (q + 1), :], float(QUADRANT * q))
        nc.vector.tensor_tensor_scan(
            out=column[:], data0=ones[:], data1=ones[:], initial=-1.0, op0=ALU.mult, op1=ALU.add
        )
        nc.vector.transpose(out=in_quadrant[:], in_=column[:, 0:QUADRANT])
        nc.vector.tensor_scalar(
            out=ident[:], in0=column[:], scalar1=quadrant_start[:], scalar2=in_quadrant[:, 0:1],
            op0=ALU.subtract, op1=ALU.is_equal,
        )

        nc.sync.dma_start(offsets[:], offs)
        nc.sync.dma_start(out=xt_w[:].bitcast(I32), in_=xt_words[0].rearrange("p n r -> p (n r)").bitcast(I32))
        load_scale_rows(nc.sync, wc_s[:], wc_scales, range(0, 2))
        load_scale_rows(nc.scalar, wc_s[:], wc_scales, range(2, 4))
        nc.sync.dma_start(out=wc_w[:].bitcast(I32), in_=wc_words[0].bitcast(I32))
        load_scale_rows(nc.scalar, xt_s, xt_scales, range(0, 3))
        load_scale_rows(nc.sync, xt_s, xt_scales, range(3, 4))
        nc.sync.dma_start(out=ws_w[:].bitcast(I32), in_=ws_words[0].bitcast(I32))
        load_scale_rows(nc.scalar, ws_s, ws_scales, range(0, 2))
        load_scale_rows(nc.sync, ws_s, ws_scales, range(2, 4))
        nc.sync.dma_start(out=wo_w[:].bitcast(I32), in_=wo_words[0].rearrange("p n r -> p (n r)").bitcast(I32))
        load_scale_rows(nc.gpsimd, wo_s, wo_scales, range(0, 2))
        load_scale_rows(nc.sync, wo_s, wo_scales, range(2, 4))

        nc.vector.tensor_copy(got_s[:], wc_s[:].indirect(offsets[:]))
        halves = [slice(0, J // 2), slice(J // 2, J)]
        for half in halves:
            list_columns = slice(half.start // ENTRIES_PER_COLUMN, half.stop // ENTRIES_PER_COLUMN)
            nc.vector.tensor_copy(got_w[:, half], wc_w[:].indirect(offsets[:, list_columns]))

        fj_turned = psum.tile([P, PACK, P], F32, name="fj_turned", tag=FACTOR_BANK)
        for i in range(PACK):
            nc.tensor.transpose(fj_turned[:, i, :], fj_col[:, i : i + 1].to_broadcast([P, P]), ident[:])
        fj_row = keep.tile([P, J], F32, name="fj_row", tag="table", align_bytes=MX_ALIGN)
        nc.vector.tensor_copy(
            out=fj_row[:].rearrange("p (u m e) -> p u m e", u=2, e=2),
            in_=fj_turned[:].rearrange("p (u e) m -> p u m e", u=2),
        )

        result_parts = (
            [(range(0, 4), "result0", nc.scalar.copy, nc.sync)],
            [(range(0, 4), "result1", nc.vector.tensor_copy, nc.sync)],
            [(range(0, 2), "shared", nc.scalar.copy, nc.sync), (range(2, 4), "score2", nc.scalar.copy, nc.sync)],
            [(range(0, 2), "score1", nc.scalar.copy, nc.sync), (range(2, 4), "result3", nc.vector.tensor_copy, nc.scalar)],
        )
        out_view = out.rearrange("(g p) t -> p g t", p=P)
        exps, inverse_sums, interleaved, result_banks = {}, {}, {}, {}

        def exponentiate(b):
            scores = psum.tile([P, J], F32, name="scores%d" % b, tag=SCORE_BANKS[b])
            tokens = slice(b * P, (b + 1) * P)
            for half in halves:
                nc.tensor.matmul_mx(
                    out=scores[:, half], lhsT=xt_w[:, tokens].bitcast(FP8X4), lhsT_scale=xt_s[:, tokens],
                    rhs=got_w[:, half].bitcast(FP4X4), rhs_scale=got_s[:, half], start=True, stop=True,
                )
            neg_max = keep.tile([P, 1], F32, name="neg_max%d" % b)
            nc.vector.tensor_reduce(out=neg_max[:], in_=scores[:], axis=AXIS.X, op=ALU.max, negate=True)
            exps[b] = keep.tile([P, J], F32, name="exps%d" % b, tag="wide%d" % b, align_bytes=MX_ALIGN)
            total = keep.tile([P, 1], F32, name="total%d" % b)
            nc.scalar.activation(
                out=exps[b][:].rearrange("p (u m e) -> p u m e", u=2, e=2),
                in_=scores[:].rearrange("p (m u e) -> p u m e", u=2, e=2),
                func=ACT.Exp, bias=neg_max[:], accum_out=total[:],
            )
            inverse_sums[b] = keep.tile([P, 1], F32, name="inverse_sum%d" % b)
            nc.vector.reciprocal(out=inverse_sums[b][:], in_=total[:])

        def weigh_and_turn(b):
            qw = keep.tile([P, J], BF16, name="qw%d" % b, tag="wide%d" % (b + TOKEN_BLOCKS - 1), align_bytes=MX_ALIGN)
            nc.vector.scalar_tensor_tensor(
                out=qw[:], in0=exps[b][:], scalar=inverse_sums[b][:], in1=fj_row[:], op0=ALU.mult, op1=ALU.mult
            )
            turned = psum.tile([P, 2, P], F32, name="turned%d" % b, tag=TURN_BANKS[b])
            pairs = qw[:].bitcast(F32)
            for u in range(2):
                nc.tensor.transpose(turned[:, u, :], pairs[:, u * P : (u + 1) * P], ident[:])
            interleaved[b] = keep.tile([P, PACK * P], BF16, name="interleaved%d" % b, align_bytes=MX_ALIGN)
            nc.scalar.copy(
                out=interleaved[b][:].bitcast(F32).rearrange("p (t u) -> p t u", u=2),
                in_=turned[:].rearrange("p u t -> p t u"),
            )

        def multiply(b):
            tokens = slice(b * P, (b + 1) * P)
            result_banks[b] = []
            for groups, tag, copy, queue in result_parts[b]:
                bank = psum.tile([P, len(groups), P], F32, name="result%d_%d" % (b, groups[0]), tag=tag)
                for place, g in enumerate(groups):
                    rows = slice(g * P, (g + 1) * P)
                    nc.tensor.matmul_mx(
                        out=bank[:, place, :], lhsT=ws_w[:, rows].bitcast(FP4X4), lhsT_scale=ws_s[:, rows],
                        rhs=xt_w[:, tokens].bitcast(FP8X4), rhs_scale=xt_s[:, tokens],
                        start=(place == 0), stop=False,
                    )
                result_banks[b].append(bank)
            qw_w = keep.tile([P, P], U32, name="qw_w%d" % b, align_bytes=MX_ALIGN)
            qw_s = keep.tile([P, P], U8, name="qw_s%d" % b, align_bytes=MX_ALIGN)
            nc.vector.quantize_mx(out=qw_w[:].bitcast(FP8X4), scales=qw_s[:], in_=interleaved[b][:])
            for bank, (groups, tag, copy, queue) in zip(result_banks[b], result_parts[b]):
                for place, g in enumerate(groups):
                    rows = slice(g * P, (g + 1) * P)
                    nc.tensor.matmul_mx(
                        out=bank[:, place, :], lhsT=wo_w[:, rows].bitcast(FP8X4), lhsT_scale=wo_s[:, rows],
                        rhs=qw_w[:].bitcast(FP8X4), rhs_scale=qw_s[:],
                        start=False, stop=(place == len(groups) - 1),
                    )

        def store(b):
            for bank, (groups, tag, copy, queue) in zip(result_banks[b], result_parts[b]):
                staged = keep.tile([P, len(groups), P], F32, name="staged%d_%d" % (b, groups[0]))
                copy(out=staged[:], in_=bank[:])
                queue.dma_start(out=out_view[:, groups[0] : groups[-1] + 1, b * P : (b + 1) * P], in_=staged[:])

        stages = (exponentiate, weigh_and_turn, multiply, store)
        for step in range(TOKEN_BLOCKS + len(stages) - 1):
            for lag, stage in enumerate(stages):
                if 0 <= step - lag < TOKEN_BLOCKS:
                    stage(step - lag)
